import numpy as np
import ml_dtypes


def mxq(x, axis, fmt="e4m3"):
    dtype, down = {"e4m3": (ml_dtypes.float8_e4m3fn, 7), "e5m2": (ml_dtypes.float8_e5m2, 14)}[fmt]
    v = np.moveaxis(np.asarray(x, np.float32).astype(ml_dtypes.bfloat16).astype(np.float64), axis, -1)
    blocks = v.reshape(v.shape[:-1] + (-1, 32))
    amax = np.abs(blocks).max(-1, keepdims=True)
    byte = np.maximum(np.where(amax > 0, np.frexp(amax)[1] - 1 + 127, 0) - down, 1)
    scale = np.exp2(byte - 127.0)
    codes = (blocks / scale).astype(np.float32).astype(dtype).astype(np.float64)
    return np.moveaxis((codes * scale).reshape(v.shape), -1, axis)


WIDE = False


def mx_kscale(k):
    if not WIDE:
        return np.ones(k)
    levels = np.array([10, -10, 5, -5, 0])
    if k % 512:
        return np.exp2(np.random.permutation(np.resize(levels, k // 32))).repeat(32)
    a = np.empty((k // 512, 16))
    for p in range(k // 512):
        a[p, :8] = np.random.permutation(np.resize(levels, 8))
        for g in range(8):
            far = levels[np.abs(levels - a[p, g]) >= 10]
            a[p, g + 8] = far[np.random.randint(len(far))]
    return np.exp2(a.ravel()).repeat(32)


def f64(x):
    return np.asarray(x).astype(np.float64)


def striped(idx):
    return np.tile(idx.reshape(-1, 16).T, (8, 1)).astype(np.uint16)


def unstriped(offs):
    return offs[:16].T.reshape(-1).astype(np.int64)


E2M1 = np.array([0.0, 0.5, 1.0, 1.5, 2.0, 3.0, 4.0, 6.0, -0.0, -0.5, -1.0, -1.5, -2.0, -3.0, -4.0, -6.0])


def pack_weight(w, fmt):
    k, n = w.shape
    w = f64(np.asarray(w, np.float32).astype(ml_dtypes.bfloat16)).reshape(k // 32, 32, n)
    amax = np.abs(w).max(1)
    if fmt == "e4m3":
        byte = np.frexp(amax)[1] - 1 + 127 - 7
    else:
        mant, ex = np.frexp(amax / 6.0)
        byte = np.where(mant > 0.5, ex, ex - 1) + 127
    byte = np.clip(np.where(amax > 0, byte, 1), 1, 254)
    scaled = (w * np.exp2(127.0 - byte)[:, None, :]).reshape(k, n).astype(np.float32)
    by_word = np.ascontiguousarray(scaled.reshape(k // 512, 128, 4, n).transpose(0, 1, 3, 2))
    if fmt == "e4m3":
        words = by_word.astype(ml_dtypes.float8_e4m3fn).view(np.uint8)
    else:
        c = by_word.astype(ml_dtypes.float4_e2m1fn).view(np.uint8) & 0xF
        words = (c[..., 0::2] | (c[..., 1::2] << 4)).reshape(k // 512, 128, 2 * n)
    return np.ascontiguousarray(words), np.ascontiguousarray(byte.astype(np.uint8).reshape(k // 512, 16, n))


def unpack_weight(words, scales, fmt):
    g, _, n = scales.shape
    words = np.ascontiguousarray(words).reshape(g, 128, n, -1)
    if fmt == "e4m3":
        vals = words.view(ml_dtypes.float8_e4m3fn).astype(np.float64)
    else:
        nib = np.empty((g, 128, n, 4), np.uint8)
        nib[..., 0::2] = words & 0xF
        nib[..., 1::2] = words >> 4
        vals = E2M1[nib]
    vals = vals * np.repeat(np.exp2(scales.astype(np.float64) - 127.0), 8, axis=1)[..., None]
    return vals.transpose(0, 1, 3, 2).reshape(g * 512, n)


def d_relu2(v):
    return 2.0 * np.maximum(v, 0.0)


K, T, E, C, H, N = 256, 768, 6, 128, 512, 1024


def by_expert(wq, xq):
    return np.concatenate([wq[e].T @ xq[:, e * C:(e + 1) * C] for e in range(E)], axis=1)


def setup_inputs():
    n = np.random.standard_normal
    s = mx_kscale(N)[:, None]
    u = mx_kscale(H)
    dy = pack_weight(n((N, T)) * s, "e4m3")
    return {
        "dy_words": dy[0],
        "dy_scales": dy[1],
        "a": n((H, E * C)).astype(np.float32),
        "w2": (n((E, N, H)) / np.sqrt(N) / s[None] * u[None, None, :]).astype(np.float32),
        "w1": (n((E, H, K)) / np.sqrt(H) / u[None, :, None]).astype(np.float32),
        "gate": np.tile(np.random.uniform(0.2, 1.0, E * C), (H, 1)).astype(np.float32),
        "offs": striped(np.random.permutation(T)[:E * C]),
    }


def reference(dy_words, dy_scales, a, w2, w1, gate, offs):
    idx = unstriped(offs)
    gq = unpack_weight(dy_words, dy_scales, "e4m3")[:, idx]
    dh = f64(gate) * by_expert(mxq(f64(w2), 1, "e4m3"), gq)
    da = dh * d_relu2(f64(a))
    dx = by_expert(mxq(f64(w1), 1, "e4m3"), mxq(da, 0, "e4m3"))
    out = np.zeros((K, T))
    out[:, idx] = dx
    return out

@@ -1,0 +1,174 @@
+from contextlib import ExitStack
+
+import concourse.mybir as mybir
+from concourse.masks import make_identity
+
+K, T, E, C, H, N = 256, 768, 6, 128, 512, 1024
+FLOPS = 2 * E * C * H * (N + K)
+BYTES = 4 * (E * N * H + E * H * K + H * T + T + K * T) + N * T + N * T // 32 + 2 * T
+
+F32 = mybir.dt.float32
+BF16 = mybir.dt.bfloat16
+I32 = mybir.dt.int32
+U32 = mybir.dt.uint32
+U16 = mybir.dt.uint16
+U8 = mybir.dt.uint8
+FP8X4 = mybir.dt.float8_e4m3fn_x4
+COPY = mybir.ActivationFunctionType.Copy
+MAX = mybir.AluOpType.max
+MULT = mybir.AluOpType.mult
+
+P = 128
+PACK = 4
+K_PASS = P * PACK
+PASSES = N // K_PASS
+HALVES = K // P
+PER_COL = 16
+
+LOADS = [["offs"], ["dy"], ["w2",0,0], ["sc"], ["gate"], ["w2",0,1], ["w1",0], ["a",0,512], ["w2",1,0], ["w2",1,1], ["w1",1], ["w2",2,0], ["w2",2,1], ["w1",2], ["w2",3,0], ["w2",3,1], ["w1",3], ["w2",4,0], ["w2",4,1], ["w2",5,0], ["w2",5,1], ["w1",4], ["w1",5], ["a",512,768]]
+GATHER_CUTS = [0,384,768]
+W2_SPLIT = [448,320,352,96,352,96,352,96,320,192,256,192,256]
+W1_SPLIT = [32,32,32,32,96,0]
+STEPS = [["gather",0,0], ["cast2",0,0], ["quant2",0,0], ["cast2",0,1], ["cast2",1,0], ["cast1",0,0], ["mm2",0,0], ["quant2",0,1], ["mm2",0,1], ["quant2",1,0], ["quant1",0,0], ["gate",0,0], ["da",0,0], ["cast2",1,1], ["quanta",0,0], ["cast2",2,0], ["cast1",1,0], ["mm2",1,0], ["quant2",1,1], ["mm1",0,0], ["mm2",1,1], ["quant2",2,0], ["gather",1,0], ["quant1",1,0], ["gate",1,0], ["da",1,0], ["cast2",2,1], ["quanta",1,0], ["cast2",3,0], ["cast1",2,0], ["mm2",2,0], ["quant2",2,1], ["mm1",1,0], ["mm2",2,1], ["scatter",0,0], ["quant2",3,0], ["scatter",0,1], ["quant1",2,0], ["gate",2,0], ["da",2,0], ["cast2",3,1], ["quanta",2,0], ["cast2",4,0], ["cast1",3,0], ["mm2",3,0], ["quant2",3,1], ["mm1",2,0], ["mm2",3,1], ["scatter",1,0], ["quant2",4,0], ["scatter",1,1], ["quant1",3,0], ["gate",3,0], ["da",3,0], ["cast2",4,1], ["quanta",3,0], ["cast2",5,0], ["cast1",4,0], ["mm2",4,0], ["quant2",4,1], ["mm1",3,0], ["mm2",4,1], ["scatter",2,0], ["quant2",5,0], ["scatter",2,1], ["quant1",4,0], ["gate",4,0], ["da",4,0], ["cast2",5,1], ["quanta",4,0], ["cast1",5,0], ["mm2",5,0], ["quant2",5,1], ["mm1",4,0], ["mm2",5,1], ["scatter",3,0], ["scatter",3,1], ["quant1",5,0], ["gate",5,0], ["da",5,0], ["quanta",5,0], ["mm1",5,0], ["scatter",4,0], ["scatter",4,1], ["scatter",5,0], ["scatter",5,1]]
+
+
+def tile_moe_bdx_mlp_relu2_kernel(tc, dy_words, dy_scales, a, w2, w1, gate, offs, out):
+    nc = tc.nc
+    with ExitStack() as ctx:
+        keep = ctx.enter_context(tc.tile_pool(name="keep", bufs=1))
+        stage = ctx.enter_context(tc.tile_pool(name="stage", bufs=4))
+        psum = ctx.enter_context(tc.psum_pool(name="psum", bufs=2))
+
+        offsets = keep.tile([P, T // PER_COL], U16, name="offsets")
+        dy_win = keep.tile([P, PASSES, T], U32, name="dy_win", align_bytes=64)
+        sc_win = keep.tile([P, T], U8, name="sc_win", align_bytes=64)
+        g_words = keep.tile([P, PASSES, T], U32, name="g_words", align_bytes=64)
+        g_scales = keep.tile([P, T], U8, name="g_scales", align_bytes=64)
+        gate_rows = keep.tile([P, C], F32, name="gate_rows")
+        gate2 = keep.tile([P, 8], F32, name="gate2")
+        ident = keep.tile([P, P], F32, name="ident")
+        a_sb = keep.tile([P, PACK, T], F32, name="a_sb", align_bytes=64)
+        w2_raw = {(e, o): keep.tile([P, PACK, H], F32, name="w2_raw%d_%d" % (e, o), align_bytes=64) for e in range(E) for o in range(PASSES)}
+        w1_raw = [keep.tile([P, PACK, K], F32, name="w1_raw%d" % e, align_bytes=64) for e in range(E)]
+        out_sb = [keep.tile([P, T], F32, name="out_sb%d" % h, align_bytes=64) for h in range(HALVES)]
+
+        nc.gpsimd.memset(sc_win[:], 0)
+        nc.gpsimd.memset(gate_rows[:], 0.0)
+        make_identity(nc, ident[:])
+
+        def load(what):
+            if what[0] == "offs":
+                nc.sync.dma_start(offsets[:], offs)
+            elif what[0] == "dy":
+                nc.sync.dma_start(dy_win[:].bitcast(I32), dy_words.rearrange("o p t d -> p o (t d)").bitcast(I32))
+            elif what[0] == "sc":
+                for q in range(4):
+                    nc.scalar.dma_start(sc_win[32 * q : 32 * q + 4 * PASSES, :].bitcast(I32), dy_scales[:, 4 * q : 4 * q + 4, :].bitcast(I32))
+            elif what[0] == "gate":
+                nc.scalar.dma_start(gate_rows[0:8, :], gate.rearrange("h (e c) -> (h e) c", c=C)[0:8, :])
+            elif what[0] == "a":
+                nc.sync.dma_start(a_sb[:, :, what[1] : what[2]], a.rearrange("(p t) s -> p t s", t=PACK)[:, :, what[1] : what[2]])
+            elif what[0] == "w2":
+                e, o = what[1], what[2]
+                nc.sync.dma_start(w2_raw[e, o][:], w2[e, o * K_PASS : (o + 1) * K_PASS, :].rearrange("(p j) i -> p j i", j=PACK))
+            else:
+                nc.sync.dma_start(w1_raw[what[1]][:], w1[what[1]].rearrange("(p j) k -> p j k", j=PACK))
+
+        for what in LOADS:
+            load(what)
+
+        gate_t = psum.tile([P, P], F32, name="gate_t", bufs=1)
+        nc.tensor.transpose(gate_t[:], gate_rows[:], ident[:])
+        nc.scalar.activation(gate2[:], gate_t[:, 0:8], COPY, scale=2.0)
+
+        def gather(lo, hi):
+            cols = offsets[:, lo // PER_COL : hi // PER_COL]
+            for o in range(PASSES):
+                nc.vector.tensor_copy(g_words[:, o, lo:hi], dy_win[:, o, :].indirect(cols))
+            nc.vector.tensor_copy(g_scales[:, lo:hi], sc_win[:].indirect(cols))
+
+        def interleave(grouped, raw, split):
+            width = raw.shape[2]
+            dst = grouped[:].rearrange("p (c i j) -> p c j i", i=4, j=PACK)
+            src = raw[:].rearrange("p j (c i) -> p c j i", i=4)
+            if split > 0:
+                nc.vector.tensor_copy(dst[:, 0 : split // 4], src[:, 0 : split // 4])
+            if split < width:
+                nc.scalar.copy(dst[:, split // 4 : width // 4], src[:, split // 4 : width // 4])
+
+        def quantize(grouped, width, tag):
+            codes = stage.tile([P, width], U32, name=tag + "_codes", align_bytes=64)
+            scales = stage.tile([P, width], U8, name=tag + "_scales", align_bytes=64)
+            nc.vector.quantize_mx(out=codes[:].bitcast(FP8X4), scales=scales[:], in_=grouped[:])
+            return codes, scales
+
+        w2_bf, w2_q, w1_bf, w1_q, dh_ps, dh_sb, dh_t, da_bf, da_q, dx_sb = {}, {}, {}, {}, {}, {}, {}, {}, {}, {}
+
+        def step(kind, e, o):
+            slots = slice(e * C, (e + 1) * C)
+            if kind == "gather":
+                gather(GATHER_CUTS[e], GATHER_CUTS[e + 1])
+            elif kind == "cast2":
+                w2_bf[e, o] = stage.tile([P, PACK * H], BF16, name="w2_bf", align_bytes=64)
+                interleave(w2_bf[e, o], w2_raw[e, o], W2_SPLIT[PASSES * e + o])
+            elif kind == "quant2":
+                w2_q[e, o] = quantize(w2_bf[e, o], H, "w2")
+            elif kind == "mm2":
+                if o == 0:
+                    dh_ps[e] = psum.tile([P, H], F32, name="dh_ps")
+                codes, scales = w2_q[e, o]
+                nc.tensor.matmul_mx(
+                    out=dh_ps[e][:],
+                    lhsT=g_words[:, o, slots].bitcast(FP8X4),
+                    lhsT_scale=g_scales[4 * o : P, slots],
+                    rhs=codes[:].bitcast(FP8X4),
+                    rhs_scale=scales[:],
+                    start=(o == 0),
+                    stop=(o == PASSES - 1),
+                )
+            elif kind == "gate":
+                dh_sb[e] = stage.tile([P, PACK, P], F32, name="dh_sb", align_bytes=64)
+                nc.scalar.activation(dh_sb[e][:], dh_ps[e][:].rearrange("c (m t) -> c t m", t=PACK), COPY, scale=gate2[:, e : e + 1])
+                dh_t[e] = psum.tile([P, PACK, C], F32, name="dh_t")
+                for t in range(PACK):
+                    nc.tensor.transpose(dh_t[e][:, t, :], dh_sb[e][:, t, :], ident[:])
+            elif kind == "da":
+                da_bf[e] = stage.tile([P, PACK * C], BF16, name="da_bf", align_bytes=64)
+                nc.vector.scalar_tensor_tensor(
+                    out=da_bf[e][:].rearrange("p (c t) -> p c t", t=PACK),
+                    in0=a_sb[:, :, slots].rearrange("p t c -> p c t"),
+                    scalar=0.0,
+                    in1=dh_t[e][:].rearrange("p t c -> p c t"),
+                    op0=MAX,
+                    op1=MULT,
+                )
+            elif kind == "quanta":
+                da_q[e] = quantize(da_bf[e], C, "da")
+            elif kind == "cast1":
+                w1_bf[e] = stage.tile([P, PACK * K], BF16, name="w1_bf", align_bytes=64)
+                interleave(w1_bf[e], w1_raw[e], W1_SPLIT[e])
+            elif kind == "quant1":
+                w1_q[e] = quantize(w1_bf[e], K, "w1")
+            elif kind == "mm1":
+                dx_ps = psum.tile([P, HALVES, C], F32, name="dx_ps")
+                dx_sb[e] = stage.tile([P, HALVES, C], F32, name="dx_sb", align_bytes=64)
+                for h in range(HALVES):
+                    nc.tensor.matmul_mx(
+                        out=dx_ps[:, h, :],
+                        lhsT=w1_q[e][0][:, h * P : (h + 1) * P].bitcast(FP8X4),
+                        lhsT_scale=w1_q[e][1][:, h * P : (h + 1) * P],
+                        rhs=da_q[e][0][:].bitcast(FP8X4),
+                        rhs_scale=da_q[e][1][:],
+                        start=True,
+                        stop=True,
+                    )
+                nc.scalar.copy(dx_sb[e][:], dx_ps[:])
+            else:
+                cols = offsets[:, e * C // PER_COL : (e + 1) * C // PER_COL]
+                nc.vector.tensor_copy(out_sb[o][:].indirect(cols), dx_sb[e][:, o, :])
+
+        for kind, e, o in STEPS:
+            step(kind, e, o)
+
+        for h in range(HALVES):
+            nc.sync.dma_start(out[h * P : (h + 1) * P, :], out_sb[h][:])

@@ -25,11 +25,11 @@ PASSES = N // K_PASS
 HALVES = K // P
 PER_COL = 16
 
-LOADS = [["offs"], ["dy"], ["w2",0,0], ["sc"], ["gate"], ["w2",0,1], ["w1",0], ["a",0,512], ["w2",1,0], ["w2",1,1], ["w1",1], ["w2",2,0], ["w2",2,1], ["w1",2], ["w2",3,0], ["w2",3,1], ["w1",3], ["w2",4,0], ["w2",4,1], ["w2",5,0], ["w2",5,1], ["w1",4], ["w1",5], ["a",512,768]]
-GATHER_CUTS = [0,384,768]
-W2_SPLIT = [448,320,352,96,352,96,352,96,320,192,256,192,256]
-W1_SPLIT = [32,32,32,32,96,0]
-STEPS = [["gather",0,0], ["cast2",0,0], ["quant2",0,0], ["cast2",0,1], ["cast2",1,0], ["cast1",0,0], ["mm2",0,0], ["quant2",0,1], ["mm2",0,1], ["quant2",1,0], ["quant1",0,0], ["gate",0,0], ["da",0,0], ["cast2",1,1], ["quanta",0,0], ["cast2",2,0], ["cast1",1,0], ["mm2",1,0], ["quant2",1,1], ["mm1",0,0], ["mm2",1,1], ["quant2",2,0], ["gather",1,0], ["quant1",1,0], ["gate",1,0], ["da",1,0], ["cast2",2,1], ["quanta",1,0], ["cast2",3,0], ["cast1",2,0], ["mm2",2,0], ["quant2",2,1], ["mm1",1,0], ["mm2",2,1], ["scatter",0,0], ["quant2",3,0], ["scatter",0,1], ["quant1",2,0], ["gate",2,0], ["da",2,0], ["cast2",3,1], ["quanta",2,0], ["cast2",4,0], ["cast1",3,0], ["mm2",3,0], ["quant2",3,1], ["mm1",2,0], ["mm2",3,1], ["scatter",1,0], ["quant2",4,0], ["scatter",1,1], ["quant1",3,0], ["gate",3,0], ["da",3,0], ["cast2",4,1], ["quanta",3,0], ["cast2",5,0], ["cast1",4,0], ["mm2",4,0], ["quant2",4,1], ["mm1",3,0], ["mm2",4,1], ["scatter",2,0], ["quant2",5,0], ["scatter",2,1], ["quant1",4,0], ["gate",4,0], ["da",4,0], ["cast2",5,1], ["quanta",4,0], ["cast1",5,0], ["mm2",5,0], ["quant2",5,1], ["mm1",4,0], ["mm2",5,1], ["scatter",3,0], ["scatter",3,1], ["quant1",5,0], ["gate",5,0], ["da",5,0], ["quanta",5,0], ["mm1",5,0], ["scatter",4,0], ["scatter",4,1], ["scatter",5,0], ["scatter",5,1]]
+LOADS = [["offs"], ["dy"], ["w2",0,0], ["sc"], ["gate"], ["w2",0,1], ["w1",0], ["w2",1,0], ["w2",1,1], ["a",0,384], ["w1",1], ["w2",2,0], ["w2",2,1], ["w1",2], ["w2",3,0], ["w2",3,1], ["w2",4,0], ["w2",4,1], ["w2",5,0], ["w2",5,1], ["w1",3], ["a",384,768], ["w1",4], ["w1",5]]
+GATHER_CUTS = [0,256,768]
+W2_SPLIT = [128,288,352,32,352,32,352,32,384,192,224,384]
+W1_SPLIT = [96,96,96,96,128,0]
+STEPS = [["gather",0,0], ["cast2",0,1], ["cast2",0,0], ["cast1",0,0], ["quant2",0,0], ["quant2",0,1], ["cast2",1,1], ["mm2",0,0], ["quant1",0,0], ["cast2",1,0], ["cast1",1,0], ["quant2",1,0], ["gather",1,0], ["quant2",1,1], ["mm2",0,1], ["cast2",2,1], ["mm2",1,0], ["quant1",1,0], ["cast2",2,0], ["cast1",2,0], ["quant2",2,0], ["gate",0,0], ["da",0,0], ["quant2",2,1], ["mm2",1,1], ["cast2",3,1], ["mm2",2,0], ["quanta",0,0], ["quant1",2,0], ["cast2",3,0], ["cast1",3,0], ["quant2",3,0], ["gate",1,0], ["mm1",0,0], ["da",1,0], ["quant2",3,1], ["mm2",2,1], ["cast2",4,1], ["mm2",3,0], ["quanta",1,0], ["quant1",3,0], ["scatter",0,0], ["cast2",4,0], ["cast1",4,0], ["quant2",4,0], ["gate",2,0], ["mm1",1,0], ["scatter",0,1], ["da",2,0], ["quant2",4,1], ["mm2",3,1], ["cast2",5,1], ["mm2",4,0], ["quanta",2,0], ["quant1",4,0], ["scatter",1,0], ["cast2",5,0], ["cast1",5,0], ["quant2",5,0], ["gate",3,0], ["mm1",2,0], ["scatter",1,1], ["da",3,0], ["quant2",5,1], ["mm2",4,1], ["mm2",5,0], ["quanta",3,0], ["quant1",5,0], ["scatter",2,0], ["gate",4,0], ["mm1",3,0], ["scatter",2,1], ["da",4,0], ["mm2",5,1], ["quanta",4,0], ["scatter",3,0], ["gate",5,0], ["mm1",4,0], ["scatter",3,1], ["da",5,0], ["quanta",5,0], ["scatter",4,0], ["mm1",5,0], ["scatter",4,1], ["scatter",5,0], ["scatter",5,1]]
 
 
 def tile_moe_bdx_mlp_relu2_kernel(tc, dy_words, dy_scales, a, w2, w1, gate, offs, out):
@@ -48,7 +48,7 @@ def tile_moe_bdx_mlp_relu2_kernel(tc, dy_words, dy_scales, a, w2, w1, gate, offs
         gate2 = keep.tile([P, 8], F32, name="gate2")
         ident = keep.tile([P, P], F32, name="ident")
         a_sb = keep.tile([P, PACK, T], F32, name="a_sb", align_bytes=64)
-        w2_raw = {(e, o): keep.tile([P, PACK, H], F32, name="w2_raw%d_%d" % (e, o), align_bytes=64) for e in range(E) for o in range(PASSES)}
+        w2_raw = {(e, o): keep.tile([P, PACK, H], F32, name="w2_raw%d_%d" % (e, o), tag="w2_raw%d_%d" % (e, o), align_bytes=64) for e in range(E) for o in range(PASSES)}
         w1_raw = [keep.tile([P, PACK, K], F32, name="w1_raw%d" % e, align_bytes=64) for e in range(E)]
         out_sb = [keep.tile([P, T], F32, name="out_sb%d" % h, align_bytes=64) for h in range(HALVES)]
 
@@ -151,7 +151,10 @@ def tile_moe_bdx_mlp_relu2_kernel(tc, dy_words, dy_scales, a, w2, w1, gate, offs
                 w1_q[e] = quantize(w1_bf[e], K, "w1")
             elif kind == "mm1":
                 dx_ps = psum.tile([P, HALVES, C], F32, name="dx_ps")
-                dx_sb[e] = stage.tile([P, HALVES, C], F32, name="dx_sb", align_bytes=64)
+                if e < 4:
+                    dx_sb[e] = keep.tile([P, HALVES, C], F32, name="dx_sb%d" % e, tag="w2_raw%d_%d" % (e + 1, 1), align_bytes=64)
+                else:
+                    dx_sb[e] = stage.tile([P, HALVES, C], F32, name="dx_sb", align_bytes=64)
                 for h in range(HALVES):
                     nc.tensor.matmul_mx(
                         out=dx_ps[:, h, :],

@@ -24,12 +24,26 @@ K_PASS = P * PACK
 PASSES = N // K_PASS
 HALVES = K // P
 PER_COL = 16
+LAST = E - 1
 
-LOADS = [["offs"], ["dy"], ["w2",0,0], ["sc"], ["gate"], ["w2",0,1], ["w1",0], ["w2",1,0], ["w2",1,1], ["a",0,384], ["w1",1], ["w2",2,0], ["w2",2,1], ["w1",2], ["w2",3,0], ["w2",3,1], ["w2",4,0], ["w2",4,1], ["w2",5,0], ["w2",5,1], ["w1",3], ["a",384,768], ["w1",4], ["w1",5]]
+LOADS = [["offs"], ["dy"], ["w2",0,0], ["sc"], ["gate"], ["w1",0], ["a",0,384], ["w2",0,1], ["w2",1,0], ["w1",1], ["w2",1,1], ["w2",2,0], ["w1",2], ["w2",2,1], ["w2",3,0], ["w2",3,1], ["w2",4,0], ["w2",4,1], ["w2",5,0], ["w2",5,1], ["w2",5,2], ["w1",3], ["a",384,768], ["w1",4], ["w1",5,0], ["w1",5,1]]
 GATHER_CUTS = [0,256,768]
-W2_SPLIT = [128,288,352,32,352,32,352,32,384,192,224,384]
-W1_SPLIT = [96,96,96,96,128,0]
-STEPS = [["gather",0,0], ["cast2",0,1], ["cast2",0,0], ["cast1",0,0], ["quant2",0,0], ["quant2",0,1], ["cast2",1,1], ["mm2",0,0], ["quant1",0,0], ["cast2",1,0], ["cast1",1,0], ["quant2",1,0], ["gather",1,0], ["quant2",1,1], ["mm2",0,1], ["cast2",2,1], ["mm2",1,0], ["quant1",1,0], ["cast2",2,0], ["cast1",2,0], ["quant2",2,0], ["gate",0,0], ["da",0,0], ["quant2",2,1], ["mm2",1,1], ["cast2",3,1], ["mm2",2,0], ["quanta",0,0], ["quant1",2,0], ["cast2",3,0], ["cast1",3,0], ["quant2",3,0], ["gate",1,0], ["mm1",0,0], ["da",1,0], ["quant2",3,1], ["mm2",2,1], ["cast2",4,1], ["mm2",3,0], ["quanta",1,0], ["quant1",3,0], ["scatter",0,0], ["cast2",4,0], ["cast1",4,0], ["quant2",4,0], ["gate",2,0], ["mm1",1,0], ["scatter",0,1], ["da",2,0], ["quant2",4,1], ["mm2",3,1], ["cast2",5,1], ["mm2",4,0], ["quanta",2,0], ["quant1",4,0], ["scatter",1,0], ["cast2",5,0], ["cast1",5,0], ["quant2",5,0], ["gate",3,0], ["mm1",2,0], ["scatter",1,1], ["da",3,0], ["quant2",5,1], ["mm2",4,1], ["mm2",5,0], ["quanta",3,0], ["quant1",5,0], ["scatter",2,0], ["gate",4,0], ["mm1",3,0], ["scatter",2,1], ["da",4,0], ["mm2",5,1], ["quanta",4,0], ["scatter",3,0], ["gate",5,0], ["mm1",4,0], ["scatter",3,1], ["da",5,0], ["quanta",5,0], ["scatter",4,0], ["mm1",5,0], ["scatter",4,1], ["scatter",5,0], ["scatter",5,1]]
+W2_SPLIT = [448,0,128,224,128,224,128,224,96,352,128,64,416]
+W1_SPLIT = [256,256,256,128,96,0,0]
+STEPS = [["gather",0,0], ["cast2",0,0], ["quant2",0,0], ["mm2",0,0], ["cast2",0,1], ["cast1",0,0], ["cast2",1,0], ["quant2",1,0], ["quant2",0,1], ["mm2",1,0], ["cast2",1,1], ["cast1",1,0], ["mm2",0,1], ["cast2",2,0], ["gather",1,0], ["quant2",2,0], ["gate",0,0], ["quant2",1,1], ["mm2",2,0], ["cast2",2,1], ["da",0,0], ["cast1",2,0], ["mm2",1,1], ["cast2",3,0], ["quant1",0,0], ["quant2",3,0], ["quanta",0,0], ["gate",1,0], ["quant2",2,1], ["mm2",3,0], ["cast2",3,1], ["da",1,0], ["cast1",3,0], ["mm2",2,1], ["cast2",4,0], ["quant1",1,0], ["quant2",4,0], ["mm1",0,0], ["quanta",1,0], ["gate",2,0], ["quant2",3,1], ["mm2",4,0], ["cast2",4,1], ["da",2,0], ["scatter",0,0], ["scatter",0,1], ["cast1",4,0], ["mm2",3,1], ["cast2",5,0], ["quant1",2,0], ["quant2",5,0], ["mm1",1,0], ["quanta",2,0], ["gate",3,0], ["quant2",4,1], ["mm2",5,0], ["cast2",5,1], ["cast2",5,2], ["da",3,0], ["scatter",1,0], ["scatter",1,1], ["cast1",5,0], ["cast1",5,1], ["mm2",4,1], ["quant1",3,0], ["mm1",2,0], ["quanta",3,0], ["gate",4,0], ["quant2",5,1], ["quant2",5,2], ["da",4,0], ["scatter",2,0], ["scatter",2,1], ["mm2",5,1], ["mm2",5,2], ["quant1",4,0], ["mm1",3,0], ["quanta",4,0], ["gate",5,0], ["gate",5,1], ["da",5,0], ["scatter",3,0], ["scatter",3,1], ["quant1",5,0], ["quant1",5,1], ["mm1",4,0], ["quanta",5,0], ["scatter",4,0], ["scatter",4,1], ["mm1",5,0], ["mm1",5,1], ["scatter",5,0], ["scatter",5,1]]
+AFTER = {"da0":"c211","da1":"c221","da2":"c231","da3":"c241","gate4":"c251"}
+
+
+def w2_piece(e, j):
+    if e == LAST and j > 0 and True:
+        return 1, (j - 1) * H // 2, H // 2
+    return j, 0, H
+
+
+def w1_piece(e, j):
+    if e == LAST and True:
+        return j * P, P
+    return 0, K
 
 
 def tile_moe_bdx_mlp_relu2_kernel(tc, dy_words, dy_scales, a, w2, w1, gate, offs, out):
@@ -48,9 +62,8 @@ def tile_moe_bdx_mlp_relu2_kernel(tc, dy_words, dy_scales, a, w2, w1, gate, offs
         gate2 = keep.tile([P, 8], F32, name="gate2")
         ident = keep.tile([P, P], F32, name="ident")
         a_sb = keep.tile([P, PACK, T], F32, name="a_sb", align_bytes=64)
-        w2_raw = {(e, o): keep.tile([P, PACK, H], F32, name="w2_raw%d_%d" % (e, o), tag="w2_raw%d_%d" % (e, o), align_bytes=64) for e in range(E) for o in range(PASSES)}
-        w1_raw = [keep.tile([P, PACK, K], F32, name="w1_raw%d" % e, align_bytes=64) for e in range(E)]
         out_sb = [keep.tile([P, T], F32, name="out_sb%d" % h, align_bytes=64) for h in range(HALVES)]
+        w2_raw, w1_raw = {}, {}
 
         nc.gpsimd.memset(sc_win[:], 0)
         nc.gpsimd.memset(gate_rows[:], 0.0)
@@ -69,10 +82,15 @@ def tile_moe_bdx_mlp_relu2_kernel(tc, dy_words, dy_scales, a, w2, w1, gate, offs
             elif what[0] == "a":
                 nc.sync.dma_start(a_sb[:, :, what[1] : what[2]], a.rearrange("(p t) s -> p t s", t=PACK)[:, :, what[1] : what[2]])
             elif what[0] == "w2":
-                e, o = what[1], what[2]
-                nc.sync.dma_start(w2_raw[e, o][:], w2[e, o * K_PASS : (o + 1) * K_PASS, :].rearrange("(p j) i -> p j i", j=PACK))
+                e, j = what[1], what[2]
+                o, lo, width = w2_piece(e, j)
+                w2_raw[e, j] = keep.tile([P, PACK, width], F32, name="c2%d%d" % (e, j), tag="c2%d%d" % (e, j), align_bytes=64)
+                nc.sync.dma_start(w2_raw[e, j][:], w2[e, o * K_PASS : (o + 1) * K_PASS, lo : lo + width].rearrange("(p j) i -> p j i", j=PACK))
             else:
-                nc.sync.dma_start(w1_raw[what[1]][:], w1[what[1]].rearrange("(p j) k -> p j k", j=PACK))
+                e, j = what[1], what[2] if len(what) > 2 else 0
+                lo, width = w1_piece(e, j)
+                w1_raw[e, j] = keep.tile([P, PACK, width], F32, name="c1%d_%d" % (e, j), tag="c1%d" % e if j == 0 else "c1x", align_bytes=64)
+                nc.sync.dma_start(w1_raw[e, j][:], w1[e, :, lo : lo + width].rearrange("(p j) k -> p j k", j=PACK))
 
         for what in LOADS:
             load(what)
@@ -80,6 +98,11 @@ def tile_moe_bdx_mlp_relu2_kernel(tc, dy_words, dy_scales, a, w2, w1, gate, offs
         gate_t = psum.tile([P, P], F32, name="gate_t", bufs=1)
         nc.tensor.transpose(gate_t[:], gate_rows[:], ident[:])
         nc.scalar.activation(gate2[:], gate_t[:, 0:8], COPY, scale=2.0)
+
+        def staged(shape, dtype, name, key):
+            if key in AFTER:
+                return keep.tile(shape, dtype, name=name + key, tag=AFTER[key], align_bytes=64)
+            return stage.tile(shape, dtype, name=name, align_bytes=64)
 
         def gather(lo, hi):
             cols = offsets[:, lo // PER_COL : hi // PER_COL]
@@ -89,6 +112,7 @@ def tile_moe_bdx_mlp_relu2_kernel(tc, dy_words, dy_scales, a, w2, w1, gate, offs
 
         def interleave(grouped, raw, split):
             width = raw.shape[2]
+            split = min(split, width)
             dst = grouped[:].rearrange("p (c i j) -> p c j i", i=4, j=PACK)
             src = raw[:].rearrange("p j (c i) -> p c j i", i=4)
             if split > 0:
@@ -96,44 +120,54 @@ def tile_moe_bdx_mlp_relu2_kernel(tc, dy_words, dy_scales, a, w2, w1, gate, offs
             if split < width:
                 nc.scalar.copy(dst[:, split // 4 : width // 4], src[:, split // 4 : width // 4])
 
-        def quantize(grouped, width, tag):
-            codes = stage.tile([P, width], U32, name=tag + "_codes", align_bytes=64)
+        def quantize(grouped, width, tag, key):
+            codes = staged([P, width], U32, tag + "_codes", key)
             scales = stage.tile([P, width], U8, name=tag + "_scales", align_bytes=64)
             nc.vector.quantize_mx(out=codes[:].bitcast(FP8X4), scales=scales[:], in_=grouped[:])
             return codes, scales
 
         w2_bf, w2_q, w1_bf, w1_q, dh_ps, dh_sb, dh_t, da_bf, da_q, dx_sb = {}, {}, {}, {}, {}, {}, {}, {}, {}, {}
+        split_last = True
+        split_k = True
 
-        def step(kind, e, o):
+        def step(kind, e, j):
             slots = slice(e * C, (e + 1) * C)
             if kind == "gather":
                 gather(GATHER_CUTS[e], GATHER_CUTS[e + 1])
             elif kind == "cast2":
-                w2_bf[e, o] = stage.tile([P, PACK * H], BF16, name="w2_bf", align_bytes=64)
-                interleave(w2_bf[e, o], w2_raw[e, o], W2_SPLIT[PASSES * e + o])
+                w2_bf[e, j] = staged([P, PACK * w2_piece(e, j)[2]], BF16, "w2_bf", "c2%d%d" % (e, j))
+                interleave(w2_bf[e, j], w2_raw[e, j], W2_SPLIT[PASSES * e + j])
             elif kind == "quant2":
-                w2_q[e, o] = quantize(w2_bf[e, o], H, "w2")
+                w2_q[e, j] = quantize(w2_bf[e, j], w2_piece(e, j)[2], "w2", "q2%d%d" % (e, j))
             elif kind == "mm2":
-                if o == 0:
-                    dh_ps[e] = psum.tile([P, H], F32, name="dh_ps")
-                codes, scales = w2_q[e, o]
-                nc.tensor.matmul_mx(
-                    out=dh_ps[e][:],
-                    lhsT=g_words[:, o, slots].bitcast(FP8X4),
-                    lhsT_scale=g_scales[4 * o : P, slots],
-                    rhs=codes[:].bitcast(FP8X4),
-                    rhs_scale=scales[:],
-                    start=(o == 0),
-                    stop=(o == PASSES - 1),
-                )
+                o, lo, width = w2_piece(e, j)
+                bank_width = H // 2 if e == LAST and split_last else H
+                if j == 0:
+                    dh_ps[e, 0] = psum.tile([P, bank_width], F32, name="dh_ps")
+                    if bank_width < H:
+                        dh_ps[e, 1] = psum.tile([P, bank_width], F32, name="dh_ps_hi", bufs=1)
+                codes, scales = w2_q[e, j]
+                for c0 in range(0, width, bank_width):
+                    nc.tensor.matmul_mx(
+                        out=dh_ps[e, (lo + c0) // bank_width][:],
+                        lhsT=g_words[:, o, slots].bitcast(FP8X4),
+                        lhsT_scale=g_scales[4 * o : P, slots],
+                        rhs=codes[:, c0 : c0 + bank_width].bitcast(FP8X4),
+                        rhs_scale=scales[:, c0 : c0 + bank_width],
+                        start=(o == 0),
+                        stop=(o == PASSES - 1),
+                    )
             elif kind == "gate":
-                dh_sb[e] = stage.tile([P, PACK, P], F32, name="dh_sb", align_bytes=64)
-                nc.scalar.activation(dh_sb[e][:], dh_ps[e][:].rearrange("c (m t) -> c t m", t=PACK), COPY, scale=gate2[:, e : e + 1])
-                dh_t[e] = psum.tile([P, PACK, C], F32, name="dh_t")
-                for t in range(PACK):
-                    nc.tensor.transpose(dh_t[e][:, t, :], dh_sb[e][:, t, :], ident[:])
+                if j == 0:
+                    dh_sb[e] = staged([P, PACK, P], F32, "dh_sb", "gate%d" % e)
+                m = dh_ps[e, j].shape[1] // PACK
+                nc.scalar.activation(dh_sb[e][:, :, j * m : (j + 1) * m], dh_ps[e, j][:].rearrange("c (m t) -> c t m", t=PACK), COPY, scale=gate2[:, e : e + 1])
+                if (j + 1) * m == P:
+                    dh_t[e] = psum.tile([P, PACK, C], F32, name="dh_t")
+                    for t in range(PACK):
+                        nc.tensor.transpose(dh_t[e][:, t, :], dh_sb[e][:, t, :], ident[:])
             elif kind == "da":
-                da_bf[e] = stage.tile([P, PACK * C], BF16, name="da_bf", align_bytes=64)
+                da_bf[e] = staged([P, PACK * C], BF16, "da_bf", "da%d" % e)
                 nc.vector.scalar_tensor_tensor(
                     out=da_bf[e][:].rearrange("p (c t) -> p c t", t=PACK),
                     in0=a_sb[:, :, slots].rearrange("p t c -> p c t"),
@@ -143,35 +177,34 @@ def tile_moe_bdx_mlp_relu2_kernel(tc, dy_words, dy_scales, a, w2, w1, gate, offs
                     op1=MULT,
                 )
             elif kind == "quanta":
-                da_q[e] = quantize(da_bf[e], C, "da")
+                da_q[e] = quantize(da_bf[e], C, "da", "qa%d" % e)
             elif kind == "cast1":
-                w1_bf[e] = stage.tile([P, PACK * K], BF16, name="w1_bf", align_bytes=64)
-                interleave(w1_bf[e], w1_raw[e], W1_SPLIT[e])
+                w1_bf[e, j] = staged([P, PACK * w1_piece(e, j)[1]], BF16, "w1_bf", "c1%d" % e)
+                interleave(w1_bf[e, j], w1_raw[e, j], W1_SPLIT[e + j])
             elif kind == "quant1":
-                w1_q[e] = quantize(w1_bf[e], K, "w1")
+                w1_q[e, j] = quantize(w1_bf[e, j], w1_piece(e, j)[1], "w1", "q1%d" % e)
             elif kind == "mm1":
-                dx_ps = psum.tile([P, HALVES, C], F32, name="dx_ps")
-                if e < 4:
-                    dx_sb[e] = keep.tile([P, HALVES, C], F32, name="dx_sb%d" % e, tag="w2_raw%d_%d" % (e + 1, 1), align_bytes=64)
-                else:
-                    dx_sb[e] = stage.tile([P, HALVES, C], F32, name="dx_sb", align_bytes=64)
-                for h in range(HALVES):
+                lo, width = w1_piece(e, j)
+                dx_ps = psum.tile([P, width // P, C], F32, name="dx_ps")
+                dx = staged([P, width // P, C], F32, "dx_sb", "ev%d" % e)
+                for h in range(width // P):
                     nc.tensor.matmul_mx(
                         out=dx_ps[:, h, :],
-                        lhsT=w1_q[e][0][:, h * P : (h + 1) * P].bitcast(FP8X4),
-                        lhsT_scale=w1_q[e][1][:, h * P : (h + 1) * P],
+                        lhsT=w1_q[e, j][0][:, h * P : (h + 1) * P].bitcast(FP8X4),
+                        lhsT_scale=w1_q[e, j][1][:, h * P : (h + 1) * P],
                         rhs=da_q[e][0][:].bitcast(FP8X4),
                         rhs_scale=da_q[e][1][:],
                         start=True,
                         stop=True,
                     )
-                nc.scalar.copy(dx_sb[e][:], dx_ps[:])
+                    dx_sb[e, lo // P + h] = dx[:, h, :]
+                nc.scalar.copy(dx[:], dx_ps[:])
             else:
                 cols = offsets[:, e * C // PER_COL : (e + 1) * C // PER_COL]
-                nc.vector.tensor_copy(out_sb[o][:].indirect(cols), dx_sb[e][:, o, :])
+                nc.vector.tensor_copy(out_sb[j][:].indirect(cols), dx_sb[e, j])
 
-        for kind, e, o in STEPS:
-            step(kind, e, o)
+        for kind, e, j in STEPS:
+            step(kind, e, j)
 
         for h in range(HALVES):
             nc.sync.dma_start(out[h * P : (h + 1) * P, :], out_sb[h][:])

@@ -28,8 +28,8 @@ LAST = E - 1
 
 LOADS = [["offs"], ["dy"], ["w2",0,0], ["sc"], ["gate"], ["w1",0], ["a",0,384], ["w2",0,1], ["w2",1,0], ["w1",1], ["w2",1,1], ["w2",2,0], ["w1",2], ["w2",2,1], ["w2",3,0], ["w2",3,1], ["w2",4,0], ["w2",4,1], ["w2",5,0], ["w2",5,1], ["w2",5,2], ["w1",3], ["a",384,768], ["w1",4], ["w1",5,0], ["w1",5,1]]
 GATHER_CUTS = [0,256,768]
-W2_SPLIT = [448,0,128,224,128,224,128,224,96,352,128,64,416]
-W1_SPLIT = [256,256,256,128,96,0,0]
+W2_SPLIT = [192,0,128,224,128,224,128,224,96,288,128,64,256]
+W1_SPLIT = [64,64,64,64,64,0,0]
 STEPS = [["gather",0,0], ["cast2",0,0], ["quant2",0,0], ["mm2",0,0], ["cast2",0,1], ["cast1",0,0], ["cast2",1,0], ["quant2",1,0], ["quant2",0,1], ["mm2",1,0], ["cast2",1,1], ["cast1",1,0], ["mm2",0,1], ["cast2",2,0], ["gather",1,0], ["quant2",2,0], ["gate",0,0], ["quant2",1,1], ["mm2",2,0], ["cast2",2,1], ["da",0,0], ["cast1",2,0], ["mm2",1,1], ["cast2",3,0], ["quant1",0,0], ["quant2",3,0], ["quanta",0,0], ["gate",1,0], ["quant2",2,1], ["mm2",3,0], ["cast2",3,1], ["da",1,0], ["cast1",3,0], ["mm2",2,1], ["cast2",4,0], ["quant1",1,0], ["quant2",4,0], ["mm1",0,0], ["quanta",1,0], ["gate",2,0], ["quant2",3,1], ["mm2",4,0], ["cast2",4,1], ["da",2,0], ["scatter",0,0], ["scatter",0,1], ["cast1",4,0], ["mm2",3,1], ["cast2",5,0], ["quant1",2,0], ["quant2",5,0], ["mm1",1,0], ["quanta",2,0], ["gate",3,0], ["quant2",4,1], ["mm2",5,0], ["cast2",5,1], ["cast2",5,2], ["da",3,0], ["scatter",1,0], ["scatter",1,1], ["cast1",5,0], ["cast1",5,1], ["mm2",4,1], ["quant1",3,0], ["mm1",2,0], ["quanta",3,0], ["gate",4,0], ["quant2",5,1], ["quant2",5,2], ["da",4,0], ["scatter",2,0], ["scatter",2,1], ["mm2",5,1], ["mm2",5,2], ["quant1",4,0], ["mm1",3,0], ["quanta",4,0], ["gate",5,0], ["gate",5,1], ["da",5,0], ["scatter",3,0], ["scatter",3,1], ["quant1",5,0], ["quant1",5,1], ["mm1",4,0], ["quanta",5,0], ["scatter",4,0], ["scatter",4,1], ["mm1",5,0], ["mm1",5,1], ["scatter",5,0], ["scatter",5,1]]
 AFTER = {"da0":"c211","da1":"c221","da2":"c231","da3":"c241","gate4":"c251"}
 

@@ -26,7 +26,7 @@ HALVES = K // P
 PER_COL = 16
 LAST = E - 1
 
-LOADS = [["offs"], ["dy"], ["w2",0,0], ["sc"], ["gate"], ["w1",0], ["a",0,384], ["w2",0,1], ["w2",1,0], ["w1",1], ["w2",1,1], ["w2",2,0], ["w1",2], ["w2",2,1], ["w2",3,0], ["w2",3,1], ["w2",4,0], ["w2",4,1], ["w2",5,0], ["w2",5,1], ["w2",5,2], ["w1",3], ["a",384,768], ["w1",4], ["w1",5,0], ["w1",5,1]]
+LOADS = [["offs"], ["dy"], ["w2",0,0], ["sc"], ["gate"], ["w1",0], ["a",0,512], ["w2",0,1], ["w2",1,0], ["w1",1], ["w2",1,1], ["w2",2,0], ["w1",2], ["w2",2,1], ["w2",3,0], ["w1",3], ["w2",3,1], ["w2",4,0], ["w2",4,1], ["w2",5,0], ["w2",5,1], ["w2",5,2], ["a",512,768], ["w1",4], ["w1",5,0], ["w1",5,1]]
 GATHER_CUTS = [0,256,768]
 W2_SPLIT = [192,0,128,224,128,224,128,224,96,288,128,64,256]
 W1_SPLIT = [64,64,64,64,64,0,0]

from contextlib import ExitStack

import concourse.mybir as mybir
from concourse.masks import make_identity

K, T, E, C, H, N = 256, 768, 6, 128, 512, 1024
FLOPS = 2 * E * C * H * (N + K)
BYTES = 4 * (E * N * H + E * H * K + H * T + T + K * T) + N * T + N * T // 32 + 2 * T

F32 = mybir.dt.float32
BF16 = mybir.dt.bfloat16
I32 = mybir.dt.int32
U32 = mybir.dt.uint32
U16 = mybir.dt.uint16
U8 = mybir.dt.uint8
FP8X4 = mybir.dt.float8_e4m3fn_x4
COPY = mybir.ActivationFunctionType.Copy
MAX = mybir.AluOpType.max
MULT = mybir.AluOpType.mult

P = 128
PACK = 4
K_PASS = P * PACK
PASSES = N // K_PASS
HALVES = K // P
PER_COL = 16
LAST = E - 1

LOADS = [["offs"], ["dy"], ["w2",0,0], ["sc"], ["gate"], ["w1",0], ["a",0,512], ["w2",0,1], ["w2",1,0], ["w1",1], ["w2",1,1], ["w2",2,0], ["w1",2], ["w2",2,1], ["w2",3,0], ["w1",3], ["w2",3,1], ["w2",4,0], ["w2",4,1], ["w2",5,0], ["w2",5,1], ["w2",5,2], ["a",512,768], ["w1",4], ["w1",5,0], ["w1",5,1]]
GATHER_CUTS = [0,256,768]
W2_SPLIT = [192,0,128,224,128,224,128,224,96,288,128,64,256]
W1_SPLIT = [64,64,64,64,64,0,0]
STEPS = [["gather",0,0], ["cast2",0,0], ["quant2",0,0], ["mm2",0,0], ["cast2",0,1], ["cast1",0,0], ["cast2",1,0], ["quant2",1,0], ["quant2",0,1], ["mm2",1,0], ["cast2",1,1], ["cast1",1,0], ["mm2",0,1], ["cast2",2,0], ["gather",1,0], ["quant2",2,0], ["gate",0,0], ["quant2",1,1], ["mm2",2,0], ["cast2",2,1], ["da",0,0], ["cast1",2,0], ["mm2",1,1], ["cast2",3,0], ["quant1",0,0], ["quant2",3,0], ["quanta",0,0], ["gate",1,0], ["quant2",2,1], ["mm2",3,0], ["cast2",3,1], ["da",1,0], ["cast1",3,0], ["mm2",2,1], ["cast2",4,0], ["quant1",1,0], ["quant2",4,0], ["mm1",0,0], ["quanta",1,0], ["gate",2,0], ["quant2",3,1], ["mm2",4,0], ["cast2",4,1], ["da",2,0], ["scatter",0,0], ["scatter",0,1], ["cast1",4,0], ["mm2",3,1], ["cast2",5,0], ["quant1",2,0], ["quant2",5,0], ["mm1",1,0], ["quanta",2,0], ["gate",3,0], ["quant2",4,1], ["mm2",5,0], ["cast2",5,1], ["cast2",5,2], ["da",3,0], ["scatter",1,0], ["scatter",1,1], ["cast1",5,0], ["cast1",5,1], ["mm2",4,1], ["quant1",3,0], ["mm1",2,0], ["quanta",3,0], ["gate",4,0], ["quant2",5,1], ["quant2",5,2], ["da",4,0], ["scatter",2,0], ["scatter",2,1], ["mm2",5,1], ["mm2",5,2], ["quant1",4,0], ["mm1",3,0], ["quanta",4,0], ["gate",5,0], ["gate",5,1], ["da",5,0], ["scatter",3,0], ["scatter",3,1], ["quant1",5,0], ["quant1",5,1], ["mm1",4,0], ["quanta",5,0], ["scatter",4,0], ["scatter",4,1], ["mm1",5,0], ["mm1",5,1], ["scatter",5,0], ["scatter",5,1]]
AFTER = {"da0":"c211","da1":"c221","da2":"c231","da3":"c241","gate4":"c251"}


def w2_piece(e, j):
    if e == LAST and j > 0 and True:
        return 1, (j - 1) * H // 2, H // 2
    return j, 0, H


def w1_piece(e, j):
    if e == LAST and True:
        return j * P, P
    return 0, K


def tile_moe_bdx_mlp_relu2_kernel(tc, dy_words, dy_scales, a, w2, w1, gate, offs, out):
    nc = tc.nc
    with ExitStack() as ctx:
        keep = ctx.enter_context(tc.tile_pool(name="keep", bufs=1))
        stage = ctx.enter_context(tc.tile_pool(name="stage", bufs=4))
        psum = ctx.enter_context(tc.psum_pool(name="psum", bufs=2))

        offsets = keep.tile([P, T // PER_COL], U16, name="offsets")
        dy_win = keep.tile([P, PASSES, T], U32, name="dy_win", align_bytes=64)
        sc_win = keep.tile([P, T], U8, name="sc_win", align_bytes=64)
        g_words = keep.tile([P, PASSES, T], U32, name="g_words", align_bytes=64)
        g_scales = keep.tile([P, T], U8, name="g_scales", align_bytes=64)
        gate_rows = keep.tile([P, C], F32, name="gate_rows")
        gate2 = keep.tile([P, 8], F32, name="gate2")
        ident = keep.tile([P, P], F32, name="ident")
        a_sb = keep.tile([P, PACK, T], F32, name="a_sb", align_bytes=64)
        out_sb = [keep.tile([P, T], F32, name="out_sb%d" % h, align_bytes=64) for h in range(HALVES)]
        w2_raw, w1_raw = {}, {}

        nc.gpsimd.memset(sc_win[:], 0)
        nc.gpsimd.memset(gate_rows[:], 0.0)
        make_identity(nc, ident[:])

        def load(what):
            if what[0] == "offs":
                nc.sync.dma_start(offsets[:], offs)
            elif what[0] == "dy":
                nc.sync.dma_start(dy_win[:].bitcast(I32), dy_words.rearrange("o p t d -> p o (t d)").bitcast(I32))
            elif what[0] == "sc":
                for q in range(4):
                    nc.scalar.dma_start(sc_win[32 * q : 32 * q + 4 * PASSES, :].bitcast(I32), dy_scales[:, 4 * q : 4 * q + 4, :].bitcast(I32))
            elif what[0] == "gate":
                nc.scalar.dma_start(gate_rows[0:8, :], gate.rearrange("h (e c) -> (h e) c", c=C)[0:8, :])
            elif what[0] == "a":
                nc.sync.dma_start(a_sb[:, :, what[1] : what[2]], a.rearrange("(p t) s -> p t s", t=PACK)[:, :, what[1] : what[2]])
            elif what[0] == "w2":
                e, j = what[1], what[2]
                o, lo, width = w2_piece(e, j)
                w2_raw[e, j] = keep.tile([P, PACK, width], F32, name="c2%d%d" % (e, j), tag="c2%d%d" % (e, j), align_bytes=64)
                nc.sync.dma_start(w2_raw[e, j][:], w2[e, o * K_PASS : (o + 1) * K_PASS, lo : lo + width].rearrange("(p j) i -> p j i", j=PACK))
            else:
                e, j = what[1], what[2] if len(what) > 2 else 0
                lo, width = w1_piece(e, j)
                w1_raw[e, j] = keep.tile([P, PACK, width], F32, name="c1%d_%d" % (e, j), tag="c1%d" % e if j == 0 else "c1x", align_bytes=64)
                nc.sync.dma_start(w1_raw[e, j][:], w1[e, :, lo : lo + width].rearrange("(p j) k -> p j k", j=PACK))

        for what in LOADS:
            load(what)

        gate_t = psum.tile([P, P], F32, name="gate_t", bufs=1)
        nc.tensor.transpose(gate_t[:], gate_rows[:], ident[:])
        nc.scalar.activation(gate2[:], gate_t[:, 0:8], COPY, scale=2.0)

        def staged(shape, dtype, name, key):
            if key in AFTER:
                return keep.tile(shape, dtype, name=name + key, tag=AFTER[key], align_bytes=64)
            return stage.tile(shape, dtype, name=name, align_bytes=64)

        def gather(lo, hi):
            cols = offsets[:, lo // PER_COL : hi // PER_COL]
            for o in range(PASSES):
                nc.vector.tensor_copy(g_words[:, o, lo:hi], dy_win[:, o, :].indirect(cols))
            nc.vector.tensor_copy(g_scales[:, lo:hi], sc_win[:].indirect(cols))

        def interleave(grouped, raw, split):
            width = raw.shape[2]
            split = min(split, width)
            dst = grouped[:].rearrange("p (c i j) -> p c j i", i=4, j=PACK)
            src = raw[:].rearrange("p j (c i) -> p c j i", i=4)
            if split > 0:
                nc.vector.tensor_copy(dst[:, 0 : split // 4], src[:, 0 : split // 4])
            if split < width:
                nc.scalar.copy(dst[:, split // 4 : width // 4], src[:, split // 4 : width // 4])

        def quantize(grouped, width, tag, key):
            codes = staged([P, width], U32, tag + "_codes", key)
            scales = stage.tile([P, width], U8, name=tag + "_scales", align_bytes=64)
            nc.vector.quantize_mx(out=codes[:].bitcast(FP8X4), scales=scales[:], in_=grouped[:])
            return codes, scales

        w2_bf, w2_q, w1_bf, w1_q, dh_ps, dh_sb, dh_t, da_bf, da_q, dx_sb = {}, {}, {}, {}, {}, {}, {}, {}, {}, {}
        split_last = True
        split_k = True

        def step(kind, e, j):
            slots = slice(e * C, (e + 1) * C)
            if kind == "gather":
                gather(GATHER_CUTS[e], GATHER_CUTS[e + 1])
            elif kind == "cast2":
                w2_bf[e, j] = staged([P, PACK * w2_piece(e, j)[2]], BF16, "w2_bf", "c2%d%d" % (e, j))
                interleave(w2_bf[e, j], w2_raw[e, j], W2_SPLIT[PASSES * e + j])
            elif kind == "quant2":
                w2_q[e, j] = quantize(w2_bf[e, j], w2_piece(e, j)[2], "w2", "q2%d%d" % (e, j))
            elif kind == "mm2":
                o, lo, width = w2_piece(e, j)
                bank_width = H // 2 if e == LAST and split_last else H
                if j == 0:
                    dh_ps[e, 0] = psum.tile([P, bank_width], F32, name="dh_ps")
                    if bank_width < H:
                        dh_ps[e, 1] = psum.tile([P, bank_width], F32, name="dh_ps_hi", bufs=1)
                codes, scales = w2_q[e, j]
                for c0 in range(0, width, bank_width):
                    nc.tensor.matmul_mx(
                        out=dh_ps[e, (lo + c0) // bank_width][:],
                        lhsT=g_words[:, o, slots].bitcast(FP8X4),
                        lhsT_scale=g_scales[4 * o : P, slots],
                        rhs=codes[:, c0 : c0 + bank_width].bitcast(FP8X4),
                        rhs_scale=scales[:, c0 : c0 + bank_width],
                        start=(o == 0),
                        stop=(o == PASSES - 1),
                    )
            elif kind == "gate":
                if j == 0:
                    dh_sb[e] = staged([P, PACK, P], F32, "dh_sb", "gate%d" % e)
                m = dh_ps[e, j].shape[1] // PACK
                nc.scalar.activation(dh_sb[e][:, :, j * m : (j + 1) * m], dh_ps[e, j][:].rearrange("c (m t) -> c t m", t=PACK), COPY, scale=gate2[:, e : e + 1])
                if (j + 1) * m == P:
                    dh_t[e] = psum.tile([P, PACK, C], F32, name="dh_t")
                    for t in range(PACK):
                        nc.tensor.transpose(dh_t[e][:, t, :], dh_sb[e][:, t, :], ident[:])
            elif kind == "da":
                da_bf[e] = staged([P, PACK * C], BF16, "da_bf", "da%d" % e)
                nc.vector.scalar_tensor_tensor(
                    out=da_bf[e][:].rearrange("p (c t) -> p c t", t=PACK),
                    in0=a_sb[:, :, slots].rearrange("p t c -> p c t"),
                    scalar=0.0,
                    in1=dh_t[e][:].rearrange("p t c -> p c t"),
                    op0=MAX,
                    op1=MULT,
                )
            elif kind == "quanta":
                da_q[e] = quantize(da_bf[e], C, "da", "qa%d" % e)
            elif kind == "cast1":
                w1_bf[e, j] = staged([P, PACK * w1_piece(e, j)[1]], BF16, "w1_bf", "c1%d" % e)
                interleave(w1_bf[e, j], w1_raw[e, j], W1_SPLIT[e + j])
            elif kind == "quant1":
                w1_q[e, j] = quantize(w1_bf[e, j], w1_piece(e, j)[1], "w1", "q1%d" % e)
            elif kind == "mm1":
                lo, width = w1_piece(e, j)
                dx_ps = psum.tile([P, width // P, C], F32, name="dx_ps")
                dx = staged([P, width // P, C], F32, "dx_sb", "ev%d" % e)
                for h in range(width // P):
                    nc.tensor.matmul_mx(
                        out=dx_ps[:, h, :],
                        lhsT=w1_q[e, j][0][:, h * P : (h + 1) * P].bitcast(FP8X4),
                        lhsT_scale=w1_q[e, j][1][:, h * P : (h + 1) * P],
                        rhs=da_q[e][0][:].bitcast(FP8X4),
                        rhs_scale=da_q[e][1][:],
                        start=True,
                        stop=True,
                    )
                    dx_sb[e, lo // P + h] = dx[:, h, :]
                nc.scalar.copy(dx[:], dx_ps[:])
            else:
                cols = offsets[:, e * C // PER_COL : (e + 1) * C // PER_COL]
                nc.vector.tensor_copy(out_sb[j][:].indirect(cols), dx_sb[e, j])

        for kind, e, j in STEPS:
            step(kind, e, j)

        for h in range(HALVES):
            nc.sync.dma_start(out[h * P : (h + 1) * P, :], out_sb[h][:])
